import numpy as np
import ml_dtypes

BF16 = ml_dtypes.bfloat16


def bf(x):
    return np.asarray(x, np.float32).astype(BF16)


def f32(x):
    return np.asarray(x, np.float32)


def f64(x):
    return np.asarray(x).astype(np.float64)


def striped(idx):
    return np.tile(idx.reshape(-1, 16).T, (8, 1))


S, K, M, N, E, Q = 512, 128, 512, 384, 4, 96


def setup_inputs():
    return {"base": bf(np.random.standard_normal((M, S))), "x": bf(np.random.standard_normal((K, N))), "w": bf(np.random.standard_normal((E, K, M)) / np.sqrt(K)), "b": f32(0.5 * np.random.standard_normal((M, 1))), "offs": striped(np.random.permutation(S)[:N])}


def reference(base, x, w, b, offs):
    idx = offs[:16].T.reshape(-1)
    z = f64(base).copy()
    for e in range(E):
        z[:, idx[e * Q : (e + 1) * Q]] = f64(w)[e].T @ f64(x)[:, e * Q : (e + 1) * Q]
    return np.tanh(z + f64(b))

@@ -1,0 +1,65 @@
+import concourse.mybir as mybir
+from concourse.masks import make_identity
+
+BF16, F32, U16 = mybir.dt.bfloat16, mybir.dt.float32, mybir.dt.uint16
+TANH = mybir.ActivationFunctionType.Tanh
+
+P = 128
+TOKENS = 512
+FEATURES = 512
+BLOCKS = FEATURES // P
+EXPERTS = 4
+PIECE = 96
+LISTED = EXPERTS * PIECE
+PIECE_COLS = PIECE // 16
+
+FLOPS = 2 * P * FEATURES * LISTED
+
+
+def tile_scatter_matmul_kernel(tc, base, x, w, b, offs, out):
+    nc = tc.nc
+    with (
+        tc.tile_pool(name="held", bufs=1) as held,
+        tc.psum_pool(name="psum", bufs=1) as psum,
+    ):
+        offsets = held.tile([P, LISTED // 16], U16, name="offsets")
+        nc.sync.dma_start(offsets[:], offs)
+
+        base_tiles = []
+        for a in range(BLOCKS):
+            base_tile = held.tile([P, TOKENS], BF16, name="base%d" % a)
+            nc.sync.dma_start(base_tile[:], base[a * P : (a + 1) * P, :])
+            base_tiles.append(base_tile)
+
+        x_tile = held.tile([P, LISTED], BF16, name="x_tile")
+        nc.scalar.dma_start(x_tile[:], x)
+        w_tiles = []
+        for e in range(EXPERTS):
+            w_tile = held.tile([P, FEATURES], BF16, name="w%d" % e)
+            nc.scalar.dma_start(w_tile[:], w[e])
+            w_tiles.append(w_tile)
+        bias = held.tile([P, BLOCKS], F32, name="bias")
+        with nc.allow_non_contiguous_dma(reason="one float32 bias value to a partition"):
+            nc.scalar.dma_start(bias[:], b.rearrange("(a p) o -> p (a o)", p=P))
+
+        ident = held.tile([P, P], BF16, name="ident")
+        make_identity(nc, ident[:])
+
+        windows = []
+        for a in range(BLOCKS):
+            window = psum.tile([P, TOKENS], F32, name="window%d" % a)
+            nc.tensor.matmul(window[:], ident[:], base_tiles[a][:], start=True, stop=True)
+            windows.append(window)
+
+        for a in range(BLOCKS):
+            for e in range(EXPERTS):
+                nc.tensor.matmul(
+                    windows[a][:].indirect(offsets[:, e * PIECE_COLS : (e + 1) * PIECE_COLS]),
+                    w_tiles[e][:, a * P : (a + 1) * P],
+                    x_tile[:, e * PIECE : (e + 1) * PIECE],
+                    start=True,
+                    stop=True,
+                )
+            result = held.tile([P, TOKENS], F32, name="result%d" % a)
+            nc.scalar.activation(result[:], windows[a][:], TANH, bias=bias[:, a : a + 1])
+            nc.sync.dma_start(out[a * P : (a + 1) * P, :], result[:])

@@ -22,25 +22,33 @@ def tile_scatter_matmul_kernel(tc, base, x, w, b, offs, out):
         tc.tile_pool(name="held", bufs=1) as held,
         tc.psum_pool(name="psum", bufs=1) as psum,
     ):
-        offsets = held.tile([P, LISTED // 16], U16, name="offsets")
-        nc.sync.dma_start(offsets[:], offs)
-
         base_tiles = []
         for a in range(BLOCKS):
             base_tile = held.tile([P, TOKENS], BF16, name="base%d" % a)
-            nc.sync.dma_start(base_tile[:], base[a * P : (a + 1) * P, :])
+            queue = nc.sync if a % 2 == 0 else nc.scalar
+            queue.dma_start(base_tile[:], base[a * P : (a + 1) * P, :])
             base_tiles.append(base_tile)
+
+        offsets = held.tile([P, LISTED // 16], U16, name="offsets")
+        nc.sync.dma_start(offsets[:], offs)
 
         x_tile = held.tile([P, LISTED], BF16, name="x_tile")
         nc.scalar.dma_start(x_tile[:], x)
-        w_tiles = []
-        for e in range(EXPERTS):
-            w_tile = held.tile([P, FEATURES], BF16, name="w%d" % e)
-            nc.scalar.dma_start(w_tile[:], w[e])
-            w_tiles.append(w_tile)
         bias = held.tile([P, BLOCKS], F32, name="bias")
         with nc.allow_non_contiguous_dma(reason="one float32 bias value to a partition"):
             nc.scalar.dma_start(bias[:], b.rearrange("(a p) o -> p (a o)", p=P))
+
+        w_halves = []
+        for h in range(2):
+            w_half = held.tile([P, EXPERTS, 2 * P], BF16, name="w_half%d" % h)
+            nc.sync.dma_start(
+                w_half[:], w[:, :, h * 2 * P : (h + 1) * 2 * P].rearrange("e k m -> k e m")
+            )
+            w_halves.append(w_half)
+
+        table_warmer = held.tile([P, 1], F32, name="table_warmer")
+        nc.vector.memset(table_warmer[:], 0.0)
+        nc.scalar.activation(table_warmer[:], table_warmer[:], TANH)
 
         ident = held.tile([P, P], BF16, name="ident")
         make_identity(nc, ident[:])
@@ -55,7 +63,7 @@ def tile_scatter_matmul_kernel(tc, base, x, w, b, offs, out):
             for e in range(EXPERTS):
                 nc.tensor.matmul(
                     windows[a][:].indirect(offsets[:, e * PIECE_COLS : (e + 1) * PIECE_COLS]),
-                    w_tiles[e][:, a * P : (a + 1) * P],
+                    w_halves[a // 2][:, e, (a % 2) * P : (a % 2 + 1) * P],
                     x_tile[:, e * PIECE : (e + 1) * PIECE],
                     start=True,
                     stop=True,

@@ -12,6 +12,7 @@ EXPERTS = 4
 PIECE = 96
 LISTED = EXPERTS * PIECE
 PIECE_COLS = PIECE // 16
+CLOCK_WARMERS = 4
 
 FLOPS = 2 * P * FEATURES * LISTED
 
@@ -52,6 +53,12 @@ def tile_scatter_matmul_kernel(tc, base, x, w, b, offs, out):
 
         ident = held.tile([P, P], BF16, name="ident")
         make_identity(nc, ident[:])
+
+        zeros = held.tile([P, TOKENS], BF16, name="zeros")
+        nc.vector.memset(zeros[:], 0.0)
+        idle_bank = psum.tile([P, TOKENS], F32, name="idle_bank")
+        for repeat in range(CLOCK_WARMERS):
+            nc.tensor.matmul(idle_bank[:], zeros[:, 0:P], zeros[:], start=True, stop=True)
 
         windows = []
         for a in range(BLOCKS):

@@ -6,13 +6,13 @@ TANH = mybir.ActivationFunctionType.Tanh
 
 P = 128
 TOKENS = 512
+HALF = TOKENS // 2
 FEATURES = 512
 BLOCKS = FEATURES // P
 EXPERTS = 4
 PIECE = 96
 LISTED = EXPERTS * PIECE
 PIECE_COLS = PIECE // 16
-CLOCK_WARMERS = 4
 
 FLOPS = 2 * P * FEATURES * LISTED
 
@@ -54,12 +54,6 @@ def tile_scatter_matmul_kernel(tc, base, x, w, b, offs, out):
         ident = held.tile([P, P], BF16, name="ident")
         make_identity(nc, ident[:])
 
-        zeros = held.tile([P, TOKENS], BF16, name="zeros")
-        nc.vector.memset(zeros[:], 0.0)
-        idle_bank = psum.tile([P, TOKENS], F32, name="idle_bank")
-        for repeat in range(CLOCK_WARMERS):
-            nc.tensor.matmul(idle_bank[:], zeros[:, 0:P], zeros[:], start=True, stop=True)
-
         windows = []
         for a in range(BLOCKS):
             window = psum.tile([P, TOKENS], F32, name="window%d" % a)
@@ -76,5 +70,9 @@ def tile_scatter_matmul_kernel(tc, base, x, w, b, offs, out):
                     stop=True,
                 )
             result = held.tile([P, TOKENS], F32, name="result%d" % a)
-            nc.scalar.activation(result[:], windows[a][:], TANH, bias=bias[:, a : a + 1])
-            nc.sync.dma_start(out[a * P : (a + 1) * P, :], result[:])
+            for h in range(2):
+                cols = slice(h * HALF, (h + 1) * HALF)
+                nc.scalar.activation(
+                    result[:, cols], windows[a][:, cols], TANH, bias=bias[:, a : a + 1]
+                )
+                nc.sync.dma_start(out[a * P : (a + 1) * P, cols], result[:, cols])

@@ -13,6 +13,7 @@ EXPERTS = 4
 PIECE = 96
 LISTED = EXPERTS * PIECE
 PIECE_COLS = PIECE // 16
+WARMERS = 1024 // P
 
 FLOPS = 2 * P * FEATURES * LISTED
 
@@ -46,6 +47,12 @@ def tile_scatter_matmul_kernel(tc, base, x, w, b, offs, out):
                 w_half[:], w[:, :, h * 2 * P : (h + 1) * 2 * P].rearrange("e k m -> k e m")
             )
             w_halves.append(w_half)
+
+        zeros = held.tile([P, P], BF16, name="zeros")
+        nc.vector.memset(zeros[:], 0.0)
+        unread = psum.tile([P, P], F32, name="unread")
+        for i in range(WARMERS):
+            nc.tensor.matmul(unread[:], zeros[:], zeros[:], start=True, stop=True)
 
         table_warmer = held.tile([P, 1], F32, name="table_warmer")
         nc.vector.memset(table_warmer[:], 0.0)

@@ -36,17 +36,18 @@ def tile_scatter_matmul_kernel(tc, base, x, w, b, offs, out):
 
         x_tile = held.tile([P, LISTED], BF16, name="x_tile")
         nc.scalar.dma_start(x_tile[:], x)
-        bias = held.tile([P, BLOCKS], F32, name="bias")
-        with nc.allow_non_contiguous_dma(reason="one float32 bias value to a partition"):
-            nc.scalar.dma_start(bias[:], b.rearrange("(a p) o -> p (a o)", p=P))
 
-        w_halves = []
-        for h in range(2):
-            w_half = held.tile([P, EXPERTS, 2 * P], BF16, name="w_half%d" % h)
+        w_blocks = []
+        for a in range(BLOCKS):
+            w_block = held.tile([P, EXPERTS, P], BF16, name="w_block%d" % a)
             nc.sync.dma_start(
-                w_half[:], w[:, :, h * 2 * P : (h + 1) * 2 * P].rearrange("e k m -> k e m")
+                w_block[:], w[:, :, a * P : (a + 1) * P].rearrange("e k m -> k e m")
             )
-            w_halves.append(w_half)
+            w_blocks.append(w_block)
+            if a == 0:
+                bias = held.tile([P, BLOCKS], F32, name="bias")
+                with nc.allow_non_contiguous_dma(reason="one float32 bias value to a partition"):
+                    nc.sync.dma_start(bias[:], b.rearrange("(a p) o -> p (a o)", p=P))
 
         zeros = held.tile([P, P], BF16, name="zeros")
         nc.vector.memset(zeros[:], 0.0)
@@ -71,7 +72,7 @@ def tile_scatter_matmul_kernel(tc, base, x, w, b, offs, out):
             for e in range(EXPERTS):
                 nc.tensor.matmul(
                     windows[a][:].indirect(offsets[:, e * PIECE_COLS : (e + 1) * PIECE_COLS]),
-                    w_halves[a // 2][:, e, (a % 2) * P : (a % 2 + 1) * P],
+                    w_blocks[a][:, e, :],
                     x_tile[:, e * PIECE : (e + 1) * PIECE],
                     start=True,
                     stop=True,

@@ -27,15 +27,14 @@ def tile_scatter_matmul_kernel(tc, base, x, w, b, offs, out):
         base_tiles = []
         for a in range(BLOCKS):
             base_tile = held.tile([P, TOKENS], BF16, name="base%d" % a)
-            queue = nc.sync if a % 2 == 0 else nc.scalar
-            queue.dma_start(base_tile[:], base[a * P : (a + 1) * P, :])
+            nc.sync.dma_start(base_tile[:], base[a * P : (a + 1) * P, :])
             base_tiles.append(base_tile)
 
         offsets = held.tile([P, LISTED // 16], U16, name="offsets")
         nc.sync.dma_start(offsets[:], offs)
 
         x_tile = held.tile([P, LISTED], BF16, name="x_tile")
-        nc.scalar.dma_start(x_tile[:], x)
+        nc.sync.dma_start(x_tile[:], x)
 
         w_blocks = []
         for a in range(BLOCKS):

@@ -6,7 +6,6 @@ TANH = mybir.ActivationFunctionType.Tanh
 
 P = 128
 TOKENS = 512
-HALF = TOKENS // 2
 FEATURES = 512
 BLOCKS = FEATURES // P
 EXPERTS = 4
@@ -77,8 +76,10 @@ def tile_scatter_matmul_kernel(tc, base, x, w, b, offs, out):
                     stop=True,
                 )
             result = held.tile([P, TOKENS], F32, name="result%d" % a)
-            for h in range(2):
-                cols = slice(h * HALF, (h + 1) * HALF)
+            pieces = 2 if a == BLOCKS - 1 else 1
+            width = TOKENS // pieces
+            for h in range(pieces):
+                cols = slice(h * width, (h + 1) * width)
                 nc.scalar.activation(
                     result[:, cols], windows[a][:, cols], TANH, bias=bias[:, a : a + 1]
                 )

@@ -23,11 +23,15 @@ def tile_scatter_matmul_kernel(tc, base, x, w, b, offs, out):
         tc.tile_pool(name="held", bufs=1) as held,
         tc.psum_pool(name="psum", bufs=1) as psum,
     ):
-        base_tiles = []
-        for a in range(BLOCKS):
-            base_tile = held.tile([P, TOKENS], BF16, name="base%d" % a)
-            nc.sync.dma_start(base_tile[:], base[a * P : (a + 1) * P, :])
-            base_tiles.append(base_tile)
+        base_blocks = []
+        for first, count in ((0, 1), (1, 1), (2, 2)):
+            base_tile = held.tile([P, count, TOKENS], BF16, name="base%d" % first)
+            nc.sync.dma_start(
+                base_tile[:],
+                base[first * P : (first + count) * P, :].rearrange("(a p) t -> p a t", p=P),
+            )
+            for i in range(count):
+                base_blocks.append(base_tile[:, i, :])
 
         offsets = held.tile([P, LISTED // 16], U16, name="offsets")
         nc.sync.dma_start(offsets[:], offs)
@@ -35,14 +39,20 @@ def tile_scatter_matmul_kernel(tc, base, x, w, b, offs, out):
         x_tile = held.tile([P, LISTED], BF16, name="x_tile")
         nc.sync.dma_start(x_tile[:], x)
 
-        w_blocks = []
-        for a in range(BLOCKS):
-            w_block = held.tile([P, EXPERTS, P], BF16, name="w_block%d" % a)
-            nc.sync.dma_start(
-                w_block[:], w[:, :, a * P : (a + 1) * P].rearrange("e k m -> k e m")
-            )
-            w_blocks.append(w_block)
-            if a == 0:
+        w_quarters = []
+        for h in range(BLOCKS // 2):
+            pair_of_blocks = []
+            for g in range(EXPERTS // 2):
+                quarter = held.tile([P, 2, 2 * P], BF16, name="w_quarter%d%d" % (h, g))
+                nc.sync.dma_start(
+                    quarter[:],
+                    w[2 * g : 2 * g + 2, :, h * 2 * P : (h + 1) * 2 * P].rearrange(
+                        "e k m -> k e m"
+                    ),
+                )
+                pair_of_blocks.append(quarter)
+            w_quarters.append(pair_of_blocks)
+            if h == 0:
                 bias = held.tile([P, BLOCKS], F32, name="bias")
                 with nc.allow_non_contiguous_dma(reason="one float32 bias value to a partition"):
                     nc.sync.dma_start(bias[:], b.rearrange("(a p) o -> p (a o)", p=P))
@@ -63,14 +73,14 @@ def tile_scatter_matmul_kernel(tc, base, x, w, b, offs, out):
         windows = []
         for a in range(BLOCKS):
             window = psum.tile([P, TOKENS], F32, name="window%d" % a)
-            nc.tensor.matmul(window[:], ident[:], base_tiles[a][:], start=True, stop=True)
+            nc.tensor.matmul(window[:], ident[:], base_blocks[a], start=True, stop=True)
             windows.append(window)
 
         for a in range(BLOCKS):
             for e in range(EXPERTS):
                 nc.tensor.matmul(
                     windows[a][:].indirect(offsets[:, e * PIECE_COLS : (e + 1) * PIECE_COLS]),
-                    w_blocks[a][:, e, :],
+                    w_quarters[a // 2][e // 2][:, e % 2, (a % 2) * P : (a % 2 + 1) * P],
                     x_tile[:, e * PIECE : (e + 1) * PIECE],
                     start=True,
                     stop=True,

@@ -24,7 +24,7 @@ def tile_scatter_matmul_kernel(tc, base, x, w, b, offs, out):
         tc.psum_pool(name="psum", bufs=1) as psum,
     ):
         base_blocks = []
-        for first, count in ((0, 1), (1, 1), (2, 2)):
+        for first, count in ((0, 2), (2, 2)):
             base_tile = held.tile([P, count, TOKENS], BF16, name="base%d" % first)
             nc.sync.dma_start(
                 base_tile[:],

@@ -39,23 +39,23 @@ def tile_scatter_matmul_kernel(tc, base, x, w, b, offs, out):
         x_tile = held.tile([P, LISTED], BF16, name="x_tile")
         nc.sync.dma_start(x_tile[:], x)
 
-        w_quarters = []
-        for h in range(BLOCKS // 2):
-            pair_of_blocks = []
-            for g in range(EXPERTS // 2):
-                quarter = held.tile([P, 2, 2 * P], BF16, name="w_quarter%d%d" % (h, g))
-                nc.sync.dma_start(
-                    quarter[:],
-                    w[2 * g : 2 * g + 2, :, h * 2 * P : (h + 1) * 2 * P].rearrange(
-                        "e k m -> k e m"
-                    ),
-                )
-                pair_of_blocks.append(quarter)
-            w_quarters.append(pair_of_blocks)
-            if h == 0:
-                bias = held.tile([P, BLOCKS], F32, name="bias")
-                with nc.allow_non_contiguous_dma(reason="one float32 bias value to a partition"):
-                    nc.sync.dma_start(bias[:], b.rearrange("(a p) o -> p (a o)", p=P))
+        w_low = []
+        for e in range(EXPERTS):
+            low = held.tile([P, 2 * P], BF16, name="w_low%d" % e)
+            nc.sync.dma_start(low[:], w[e, :, 0 : 2 * P])
+            w_low.append(low)
+
+        bias = held.tile([P, BLOCKS], F32, name="bias")
+        with nc.allow_non_contiguous_dma(reason="one float32 bias value to a partition"):
+            nc.sync.dma_start(bias[:], b.rearrange("(a p) o -> p (a o)", p=P))
+
+        w_high = []
+        for g in range(EXPERTS // 2):
+            high = held.tile([P, 2, 2 * P], BF16, name="w_high%d" % g)
+            nc.sync.dma_start(
+                high[:], w[2 * g : 2 * g + 2, :, 2 * P : 4 * P].rearrange("e k m -> k e m")
+            )
+            w_high.append(high)
 
         zeros = held.tile([P, P], BF16, name="zeros")
         nc.vector.memset(zeros[:], 0.0)
@@ -78,9 +78,11 @@ def tile_scatter_matmul_kernel(tc, base, x, w, b, offs, out):
 
         for a in range(BLOCKS):
             for e in range(EXPERTS):
+                block_cols = slice((a % 2) * P, (a % 2 + 1) * P)
+                weights = w_low[e][:, block_cols] if a < 2 else w_high[e // 2][:, e % 2, block_cols]
                 nc.tensor.matmul(
                     windows[a][:].indirect(offsets[:, e * PIECE_COLS : (e + 1) * PIECE_COLS]),
-                    w_quarters[a // 2][e // 2][:, e % 2, (a % 2) * P : (a % 2 + 1) * P],
+                    weights,
                     x_tile[:, e * PIECE : (e + 1) * PIECE],
                     start=True,
                     stop=True,

@@ -40,10 +40,13 @@ def tile_scatter_matmul_kernel(tc, base, x, w, b, offs, out):
         nc.sync.dma_start(x_tile[:], x)
 
         w_low = []
-        for e in range(EXPERTS):
-            low = held.tile([P, 2 * P], BF16, name="w_low%d" % e)
-            nc.sync.dma_start(low[:], w[e, :, 0 : 2 * P])
-            w_low.append(low)
+        for first, count in ((0, 2), (2, 1), (3, 1)):
+            low = held.tile([P, count, 2 * P], BF16, name="w_low%d" % first)
+            nc.sync.dma_start(
+                low[:], w[first : first + count, :, 0 : 2 * P].rearrange("e k m -> k e m")
+            )
+            for i in range(count):
+                w_low.append(low[:, i, :])
 
         bias = held.tile([P, BLOCKS], F32, name="bias")
         with nc.allow_non_contiguous_dma(reason="one float32 bias value to a partition"):
@@ -88,7 +91,7 @@ def tile_scatter_matmul_kernel(tc, base, x, w, b, offs, out):
                     stop=True,
                 )
             result = held.tile([P, TOKENS], F32, name="result%d" % a)
-            pieces = 2 if a == BLOCKS - 1 else 1
+            pieces = 2 if a in (0, BLOCKS - 1) else 1
             width = TOKENS // pieces
             for h in range(pieces):
                 cols = slice(h * width, (h + 1) * width)

import concourse.mybir as mybir
from concourse.masks import make_identity

BF16, F32, U16 = mybir.dt.bfloat16, mybir.dt.float32, mybir.dt.uint16
TANH = mybir.ActivationFunctionType.Tanh

P = 128
TOKENS = 512
FEATURES = 512
BLOCKS = FEATURES // P
EXPERTS = 4
PIECE = 96
LISTED = EXPERTS * PIECE
PIECE_COLS = PIECE // 16
WARMERS = 1024 // P

FLOPS = 2 * P * FEATURES * LISTED


def tile_scatter_matmul_kernel(tc, base, x, w, b, offs, out):
    nc = tc.nc
    with (
        tc.tile_pool(name="held", bufs=1) as held,
        tc.psum_pool(name="psum", bufs=1) as psum,
    ):
        base_blocks = []
        for first, count in ((0, 2), (2, 2)):
            base_tile = held.tile([P, count, TOKENS], BF16, name="base%d" % first)
            nc.sync.dma_start(
                base_tile[:],
                base[first * P : (first + count) * P, :].rearrange("(a p) t -> p a t", p=P),
            )
            for i in range(count):
                base_blocks.append(base_tile[:, i, :])

        offsets = held.tile([P, LISTED // 16], U16, name="offsets")
        nc.sync.dma_start(offsets[:], offs)

        x_tile = held.tile([P, LISTED], BF16, name="x_tile")
        nc.sync.dma_start(x_tile[:], x)

        w_low = []
        for first, count in ((0, 2), (2, 1), (3, 1)):
            low = held.tile([P, count, 2 * P], BF16, name="w_low%d" % first)
            nc.sync.dma_start(
                low[:], w[first : first + count, :, 0 : 2 * P].rearrange("e k m -> k e m")
            )
            for i in range(count):
                w_low.append(low[:, i, :])

        bias = held.tile([P, BLOCKS], F32, name="bias")
        with nc.allow_non_contiguous_dma(reason="one float32 bias value to a partition"):
            nc.sync.dma_start(bias[:], b.rearrange("(a p) o -> p (a o)", p=P))

        w_high = []
        for g in range(EXPERTS // 2):
            high = held.tile([P, 2, 2 * P], BF16, name="w_high%d" % g)
            nc.sync.dma_start(
                high[:], w[2 * g : 2 * g + 2, :, 2 * P : 4 * P].rearrange("e k m -> k e m")
            )
            w_high.append(high)

        zeros = held.tile([P, P], BF16, name="zeros")
        nc.vector.memset(zeros[:], 0.0)
        unread = psum.tile([P, P], F32, name="unread")
        for i in range(WARMERS):
            nc.tensor.matmul(unread[:], zeros[:], zeros[:], start=True, stop=True)

        table_warmer = held.tile([P, 1], F32, name="table_warmer")
        nc.vector.memset(table_warmer[:], 0.0)
        nc.scalar.activation(table_warmer[:], table_warmer[:], TANH)

        ident = held.tile([P, P], BF16, name="ident")
        make_identity(nc, ident[:])

        windows = []
        for a in range(BLOCKS):
            window = psum.tile([P, TOKENS], F32, name="window%d" % a)
            nc.tensor.matmul(window[:], ident[:], base_blocks[a], start=True, stop=True)
            windows.append(window)

        for a in range(BLOCKS):
            for e in range(EXPERTS):
                block_cols = slice((a % 2) * P, (a % 2 + 1) * P)
                weights = w_low[e][:, block_cols] if a < 2 else w_high[e // 2][:, e % 2, block_cols]
                nc.tensor.matmul(
                    windows[a][:].indirect(offsets[:, e * PIECE_COLS : (e + 1) * PIECE_COLS]),
                    weights,
                    x_tile[:, e * PIECE : (e + 1) * PIECE],
                    start=True,
                    stop=True,
                )
            result = held.tile([P, TOKENS], F32, name="result%d" % a)
            pieces = 2 if a in (0, BLOCKS - 1) else 1
            width = TOKENS // pieces
            for h in range(pieces):
                cols = slice(h * width, (h + 1) * width)
                nc.scalar.activation(
                    result[:, cols], windows[a][:, cols], TANH, bias=bias[:, a : a + 1]
                )
                nc.sync.dma_start(out[a * P : (a + 1) * P, cols], result[:, cols])
